import numpy as np
import ml_dtypes


def mxq(x, axis, fmt="e4m3"):
    dtype, down = {"e4m3": (ml_dtypes.float8_e4m3fn, 7), "e5m2": (ml_dtypes.float8_e5m2, 14)}[fmt]
    v = np.moveaxis(np.asarray(x, np.float32).astype(ml_dtypes.bfloat16).astype(np.float64), axis, -1)
    blocks = v.reshape(v.shape[:-1] + (-1, 32))
    amax = np.abs(blocks).max(-1, keepdims=True)
    byte = np.maximum(np.where(amax > 0, np.frexp(amax)[1] - 1 + 127, 0) - down, 1)
    scale = np.exp2(byte - 127.0)
    codes = (blocks / scale).astype(np.float32).astype(dtype).astype(np.float64)
    return np.moveaxis((codes * scale).reshape(v.shape), -1, axis)


WIDE = False


def mx_kscale(k):
    if not WIDE:
        return np.ones(k)
    levels = np.array([10, -10, 5, -5, 0])
    if k % 512:
        return np.exp2(np.random.permutation(np.resize(levels, k // 32))).repeat(32)
    a = np.empty((k // 512, 16))
    for p in range(k // 512):
        a[p, :8] = np.random.permutation(np.resize(levels, 8))
        for g in range(8):
            far = levels[np.abs(levels - a[p, g]) >= 10]
            a[p, g + 8] = far[np.random.randint(len(far))]
    return np.exp2(a.ravel()).repeat(32)


def f64(x):
    return np.asarray(x).astype(np.float64)


def striped(idx):
    return np.tile(idx.reshape(-1, 16).T, (8, 1)).astype(np.uint16)


def unstriped(offs):
    return offs[:16].T.reshape(-1).astype(np.int64)


def striped8(idx):
    return np.concatenate([x.reshape(-1, 16).T for x in idx]).astype(np.uint16)


def runs(offs, k):
    lists = np.stack([offs[16 * r : 16 * r + 16].T.reshape(-1) for r in range(8)]).astype(np.int64)
    return lists[np.arange(k) % 512 // 64]


def pack_weight(w):
    k, n = w.shape
    w = f64(np.asarray(w, np.float32).astype(ml_dtypes.bfloat16)).reshape(k // 32, 32, n)
    amax = np.abs(w).max(1)
    byte = np.clip(np.where(amax > 0, np.frexp(amax)[1] - 1 + 127 - 7, 1), 1, 254)
    scaled = (w * np.exp2(127.0 - byte)[:, None, :]).reshape(k, n).astype(np.float32)
    words = np.ascontiguousarray(scaled.reshape(k // 512, 128, 4, n).transpose(0, 1, 3, 2)).astype(ml_dtypes.float8_e4m3fn).view(np.uint8)
    return words, np.ascontiguousarray(byte.astype(np.uint8).reshape(k // 512, 16, n))


def unpack_weight(words, scales):
    g, p, n, _ = words.shape
    vals = np.ascontiguousarray(words).view(ml_dtypes.float8_e4m3fn).astype(np.float64) * np.repeat(np.exp2(scales.astype(np.float64) - 127.0), 8, axis=1)[..., None]
    return vals.transpose(0, 1, 3, 2).reshape(g * 512, n)


def relu(v):
    return np.maximum(v, 0.0)

def planes(y):
    n, m = y.shape
    v = y.astype(np.float32).astype(ml_dtypes.bfloat16).astype(np.float64).reshape(n // 32, 32, m)
    top = np.abs(v).max(1)
    byte = np.clip(np.where(top > 0, np.frexp(top)[1] - 1 + 127 - 7, 1), 1, 254)
    codes = (v * np.exp2(127.0 - byte)[:, None, :]).reshape(n, m).astype(np.float32).astype(ml_dtypes.float8_e4m3fn).view(np.uint8)
    words = codes.reshape(n // 512, 128, 4, m).transpose(0, 1, 3, 2)
    return np.ascontiguousarray(words), np.ascontiguousarray(byte.astype(np.uint8).reshape(n // 512, 16, m))


K, T, S, N, H = 512, 2048, 256, 512, 512


def setup_inputs():
    n = np.random.standard_normal
    s = mx_kscale(K)[:, None]
    u = mx_kscale(H)
    packed_xT = pack_weight(n((K, T)) * s)
    packed_w1 = pack_weight(n((K, H)) / np.sqrt(K) / s)
    packed_w2 = pack_weight(n((H, N)) / np.sqrt(H) / u[:, None])
    return {
        "x_words": packed_xT[0],
        "x_scales": packed_xT[1],
        "w1_words": packed_w1[0],
        "w1_scales": packed_w1[1],
        "gn": (np.random.uniform(0.5, 1.5, (H, 1)) * u[:, None]).astype(np.float32),
        "w2_words": packed_w2[0],
        "w2_scales": packed_w2[1],
        "offs": striped8(np.random.randint(0, T, (8, S))),
        "n1": striped(np.random.permutation(S)),
        "n2": striped(np.random.permutation(S)),
        "n3": striped(np.random.permutation(S)),
    }


def reference(x_words, x_scales, w1_words, w1_scales, gn, w2_words, w2_scales, offs, n1, n2, n3):
    xq = unpack_weight(x_words, x_scales)[np.arange(K)[:, None], runs(offs, K)]
    y = unpack_weight(w1_words, w1_scales).T @ xq
    z = f64(gn) * (y / (np.abs(y[:, unstriped(n1)]) + 0.5))
    h = unpack_weight(w2_words, w2_scales).T @ mxq(z, 0, "e4m3")
    out_0 = relu(h - h[:, unstriped(n2)]) + 0.5 * (relu(h[:, unstriped(n3)] - h))
    return (out_0,) + planes(out_0)

@@ -1,0 +1,200 @@
+from contextlib import ExitStack
+
+import concourse.mybir as mybir
+
+K, T, S, H, N = 512, 2048, 256, 512, 512
+FLOPS = 2 * K * H * S + 2 * H * N * S
+
+F32, BF16 = mybir.dt.float32, mybir.dt.bfloat16
+I32, U32, U16, U8 = mybir.dt.int32, mybir.dt.uint32, mybir.dt.uint16, mybir.dt.uint8
+FP8X4 = mybir.dt.float8_e4m3fn_x4
+ALU = mybir.AluOpType
+ACT = mybir.ActivationFunctionType
+
+P = 128
+PACK = 4
+QUADS = 4
+HALF = S // 2
+SCALAR_ABS = ()
+PIECES = 4
+PIECE = S // PIECES
+
+
+def words_of(packed):
+    return packed[0].rearrange("p n t -> p (n t)").bitcast(I32)
+
+
+def tile_picked_hashnormhinge_none_po_kernel(
+    tc, x_words, x_scales, w1_words, w1_scales, gn, w2_words, w2_scales, offs, n1, n2, n3, out_0, out_1, out_2
+):
+    nc = tc.nc
+    with ExitStack() as ctx:
+        lists = ctx.enter_context(tc.tile_pool(name="lists", bufs=1))
+        sb = ctx.enter_context(tc.tile_pool(name="sb", bufs=1))
+        psum = ctx.enter_context(tc.psum_pool(name="psum", bufs=1))
+
+        def new(shape, dtype, name, tag=None):
+            return sb.tile(shape, dtype, name=name, tag=tag or name, align_bytes=64)
+
+        offs_sb = lists.tile([P, S // 16], U16, name="offs_sb")
+        n1_sb = lists.tile([P, S // 16], U16, name="n1_sb")
+        n2_sb = lists.tile([P, S // 16], U16, name="n2_sb")
+        n3_sb = lists.tile([P, S // 16], U16, name="n3_sb")
+
+        def half_list(tile, half):
+            return tile[:, half * (HALF // 16) : (half + 1) * (HALF // 16)]
+
+        def cols(half):
+            return slice(half * HALF, (half + 1) * HALF)
+
+        def load_scale_rows(queue, tile, scales, q):
+            rows = scales[0].bitcast(I32)[4 * q : 4 * q + 4, :]
+            queue.dma_start(tile[:].bitcast(I32)[32 * q : 32 * q + 4, :], rows)
+
+        def deal(name, raw, dtype, tag=None):
+            dealt = new([P, H], dtype, name, tag=tag)
+            nc.vector.tensor_copy(
+                dealt[:].rearrange("p (t m) -> p m t", t=PACK), raw[:].rearrange("p (m t) -> p m t", t=PACK)
+            )
+            return dealt
+
+        x_table_scales = new([P, T], U8, "x_table_scales")
+        w1_raw_scales = new([P, H], U8, "w1_raw_scales")
+        x_plane = new([P, S], U8, "x_plane")
+        nc.gpsimd.memset(w1_raw_scales[:].bitcast(U32), 0)
+        nc.vector.memset(x_table_scales[:].bitcast(I32), 0)
+        nc.vector.memset(x_plane[:].bitcast(I32), 0)
+
+        nc.sync.dma_start(offs_sb[:], offs)
+        w1_raw = new([P, H], I32, "w1_raw")
+        nc.scalar.dma_start(w1_raw[:], words_of(w1_words))
+        nc.scalar.dma_start(x_table_scales[:].bitcast(I32)[0:P:8, :], x_scales[0].bitcast(I32))
+        for q in range(QUADS):
+            load_scale_rows(nc.scalar, w1_raw_scales, w1_scales, q)
+        nc.sync.dma_start(n1_sb[:], n1)
+        nc.sync.dma_start(n2_sb[:], n2)
+        nc.sync.dma_start(n3_sb[:], n3)
+        x_table = new([P, T], I32, "x_table", tag="table")
+        nc.sync.dma_start(x_table[:], words_of(x_words))
+        w2_raw_scales = new([P, N], U8, "w2_raw_scales")
+        nc.gpsimd.memset(w2_raw_scales[:].bitcast(U32), 0)
+        gn_sb = new([P, PACK], F32, "gn_sb")
+        nc.gpsimd.dma_start(gn_sb[:], gn.rearrange("(p t) o -> p (t o)", t=PACK))
+        for q in range(QUADS):
+            load_scale_rows(nc.gpsimd, w2_raw_scales, w2_scales, q)
+
+        x_picked_scales = new([P, S], U8, "x_picked_scales")
+        nc.vector.tensor_copy(x_picked_scales[:], x_table_scales[:].indirect(offs_sb[:]))
+        for q in range(QUADS):
+            nc.scalar.dma_start(
+                x_plane[:].bitcast(I32)[32 * q : 32 * q + 4, :],
+                x_picked_scales[:].bitcast(I32)[32 * q : 32 * q + 32 : 8, :],
+            )
+        w1_dealt = deal("w1_dealt", w1_raw, I32)
+        w1_plane = deal("w1_plane", w1_raw_scales, U8)
+        x_picked = new([P, S], U32, "x_picked")
+        nc.vector.tensor_copy(x_picked[:], x_table[:].bitcast(U32).indirect(offs_sb[:]))
+
+        w2_raw = new([P, N], I32, "w2_raw", tag="table")
+        nc.sync.dma_start(w2_raw[:], words_of(w2_words))
+        y = [psum.tile([P, S], F32, name="y%d" % t, tag="y%d" % t) for t in range(PACK)]
+        for t in range(PACK):
+            rows = slice(t * P, (t + 1) * P)
+            nc.tensor.matmul_mx(
+                out=y[t][:], lhsT=w1_dealt[:, rows].bitcast(FP8X4), lhsT_scale=w1_plane[:, rows],
+                rhs=x_picked[:].bitcast(FP8X4), rhs_scale=x_plane[:], start=True, stop=True,
+            )
+
+        mirror = new([P, PACK, S], F32, "mirror")
+        denom = new([P, PACK, S], F32, "denom")
+        root = new([P, PACK, S], F32, "root")
+        for t in range(PACK):
+            if t in SCALAR_ABS:
+                nc.scalar.activation(denom[:, t, :], y[t][:], ACT.Abs)
+                nc.scalar.activation(root[:, t, :], denom[:, t, :], ACT.Abs_reciprocal_sqrt, bias=0.5)
+            else:
+                nc.vector.tensor_scalar(mirror[:, t, :], y[t][:], -1.0, 0.5, ALU.mult, ALU.add)
+                nc.vector.scalar_tensor_tensor(denom[:, t, :], y[t][:], 0.5, mirror[:, t, :], ALU.add, ALU.max)
+                nc.scalar.activation(root[:, t, :], denom[:, t, :], ACT.Abs_reciprocal_sqrt)
+
+        w2_plane = deal("w2_plane", w2_raw_scales, U8, tag="mirror")
+        w2_dealt = deal("w2_dealt", w2_raw, I32, tag="denom")
+
+        h_wide = new([P, (PACK + 1) * S], F32, "h_wide")
+        nc.gpsimd.memset(h_wide[:, PACK * S :], 0.0)
+        h_sb = h_wide[:, : PACK * S].rearrange("p (t j) -> p t j", t=PACK)
+        for half in range(2):
+            root_at = new([P, PACK, HALF], F32, "root_at%d" % half)
+            part = new([P, PACK, HALF], F32, "part%d" % half)
+            for t in range(PACK):
+                nc.scalar.activation(root_at[:, t, :], root[:, t, :].indirect(half_list(n1_sb, half)), ACT.Copy)
+                nc.vector.scalar_tensor_tensor(
+                    part[:, t, :], y[t][:, cols(half)], gn_sb[:, t : t + 1], root_at[:, t, :], ALU.mult, ALU.mult
+                )
+            z_bf = new([P, HALF, PACK], BF16, "z_bf%d" % half)
+            nc.vector.tensor_tensor(
+                z_bf[:].rearrange("p (c i) t -> p c t i", i=4),
+                part[:].rearrange("p t (c i) -> p c t i", i=4),
+                root_at[:].rearrange("p t (c i) -> p c t i", i=4),
+                ALU.mult,
+            )
+            z_words = new([P, HALF], U32, "z_words%d" % half)
+            z_plane = new([P, HALF], U8, "z_plane%d" % half)
+            nc.vector.quantize_mx(
+                out=z_words[:].bitcast(FP8X4), scales=z_plane[:], in_=z_bf[:].rearrange("p j t -> p (j t)")
+            )
+            for pair in range(2):
+                bank = psum.tile([P, 2, HALF], F32, name="h%d%d" % (half, pair), tag="h%d%d" % (half, pair))
+                for e in range(2):
+                    t = 2 * pair + e
+                    rows = slice(t * P, (t + 1) * P)
+                    nc.tensor.matmul_mx(
+                        out=bank[:, e, :], lhsT=w2_dealt[:, rows].bitcast(FP8X4), lhsT_scale=w2_plane[:, rows],
+                        rhs=z_words[:].bitcast(FP8X4), rhs_scale=z_plane[:], start=True, stop=True,
+                    )
+                dest = h_sb[:, 2 * pair : 2 * pair + 2, cols(half)]
+                if half == 1 and pair == 1:
+                    nc.vector.tensor_copy(dest, bank[:])
+                else:
+                    nc.scalar.copy(dest, bank[:])
+
+        out_rows = out_0.rearrange("(p t) j -> p t j", t=PACK)
+        o_words = new([P, S], I32, "o_words")
+        o_plane = new([P, S], U8, "o_plane")
+        res = new([P, PACK, S], F32, "res")
+        res_bf = new([P, S, PACK], BF16, "res_bf")
+
+        def interleave(engine_copy, pair, js):
+            ts = slice(2 * pair, 2 * pair + 2)
+            engine_copy(res_bf[:, js, ts], res[:, ts, js].rearrange("p t j -> p j t"))
+
+        for t in range(PACK):
+            window = h_wide[:, t * S : (t + 2) * S]
+            h2 = new([P, S], F32, "h2_%d" % t)
+            h3 = new([P, S], F32, "h3_%d" % t)
+            nc.scalar.activation(h3[:], window.indirect(n3_sb[:]), ACT.Copy, scale=0.5)
+            if t == 0:
+                nc.vector.tensor_copy(h2[:], window.indirect(n2_sb[:]))
+            else:
+                nc.scalar.activation(h2[:], window.indirect(n2_sb[:]), ACT.Copy)
+            down = new([P, S], F32, "down%d" % t)
+            up = new([P, S], F32, "up%d" % t)
+            down_pos = new([P, S], F32, "down_pos%d" % t)
+            nc.vector.scalar_tensor_tensor(up[:], h_sb[:, t, :], -0.5, h3[:], ALU.mult, ALU.add)
+            nc.vector.tensor_tensor(down[:], h_sb[:, t, :], h2[:], ALU.subtract)
+            nc.vector.tensor_scalar_max(down_pos[:], up[:], 0.0)
+            nc.vector.scalar_tensor_tensor(res[:, t, :], down[:], 0.0, down_pos[:], ALU.max, ALU.add)
+            nc.sync.dma_start(out_rows[:, t, :], res[:, t, :])
+            if t == 1:
+                interleave(nc.scalar.copy, 0, slice(0, S))
+        for half in range(2):
+            interleave(nc.vector.tensor_copy, 1, cols(half))
+        for half in range(2):
+            nc.vector.quantize_mx(
+                out=o_words[:, cols(half)].bitcast(FP8X4), scales=o_plane[:, cols(half)],
+                in_=res_bf[:, cols(half), :].rearrange("p j t -> p (j t)"),
+            )
+        nc.scalar.dma_start(words_of(out_1), o_words[:])
+        for q in range(QUADS):
+            queue = nc.sync if q < 3 else nc.scalar
+            queue.dma_start(out_2[0].bitcast(I32)[4 * q : 4 * q + 4, :], o_plane[:].bitcast(I32)[32 * q : 32 * q + 4, :])

@@ -15,9 +15,6 @@ P = 128
 PACK = 4
 QUADS = 4
 HALF = S // 2
-SCALAR_ABS = ()
-PIECES = 4
-PIECE = S // PIECES
 
 
 def words_of(packed):
@@ -62,26 +59,30 @@ def tile_picked_hashnormhinge_none_po_kernel(
         w1_raw_scales = new([P, H], U8, "w1_raw_scales")
         x_plane = new([P, S], U8, "x_plane")
         nc.gpsimd.memset(w1_raw_scales[:].bitcast(U32), 0)
-        nc.vector.memset(x_table_scales[:].bitcast(I32), 0)
         nc.vector.memset(x_plane[:].bitcast(I32), 0)
 
-        nc.sync.dma_start(offs_sb[:], offs)
         w1_raw = new([P, H], I32, "w1_raw")
-        nc.scalar.dma_start(w1_raw[:], words_of(w1_words))
-        nc.scalar.dma_start(x_table_scales[:].bitcast(I32)[0:P:8, :], x_scales[0].bitcast(I32))
+        w2_raw = new([P, N], I32, "w2_raw")
+        x_table = new([P, T], I32, "x_table", tag="table")
+        gn_sb = new([P, PACK], F32, "gn_sb")
+        nc.sync.dma_start(offs_sb[:], offs)
+        nc.scalar.dma_start(
+            x_table_scales[:].bitcast(I32), x_scales[0].bitcast(I32).unsqueeze(1).to_broadcast([16, 8, T // 4])
+        )
+        nc.sync.dma_start(x_table[:], words_of(x_words))
         for q in range(QUADS):
-            load_scale_rows(nc.scalar, w1_raw_scales, w1_scales, q)
+            load_scale_rows(nc.scalar if q < 2 else nc.gpsimd, w1_raw_scales, w1_scales, q)
+        nc.scalar.dma_start(w1_raw[:], words_of(w1_words))
         nc.sync.dma_start(n1_sb[:], n1)
         nc.sync.dma_start(n2_sb[:], n2)
         nc.sync.dma_start(n3_sb[:], n3)
-        x_table = new([P, T], I32, "x_table", tag="table")
-        nc.sync.dma_start(x_table[:], words_of(x_words))
-        w2_raw_scales = new([P, N], U8, "w2_raw_scales")
-        nc.gpsimd.memset(w2_raw_scales[:].bitcast(U32), 0)
-        gn_sb = new([P, PACK], F32, "gn_sb")
-        nc.gpsimd.dma_start(gn_sb[:], gn.rearrange("(p t) o -> p (t o)", t=PACK))
-        for q in range(QUADS):
-            load_scale_rows(nc.gpsimd, w2_raw_scales, w2_scales, q)
+        nc.sync.dma_start(w2_raw[:], words_of(w2_words))
+        nc.sync.dma_start(gn_sb[:], gn.rearrange("(p t) o -> p (t o)", t=PACK))
+
+        warm_in = new([P, 1], F32, "warm_in")
+        warm_out = new([P, 1], F32, "warm_out")
+        nc.vector.memset(warm_in[:], 1.0)
+        nc.scalar.activation(warm_out[:], warm_in[:], ACT.Abs_reciprocal_sqrt)
 
         x_picked_scales = new([P, S], U8, "x_picked_scales")
         nc.vector.tensor_copy(x_picked_scales[:], x_table_scales[:].indirect(offs_sb[:]))
@@ -95,8 +96,11 @@ def tile_picked_hashnormhinge_none_po_kernel(
         x_picked = new([P, S], U32, "x_picked")
         nc.vector.tensor_copy(x_picked[:], x_table[:].bitcast(U32).indirect(offs_sb[:]))
 
-        w2_raw = new([P, N], I32, "w2_raw", tag="table")
-        nc.sync.dma_start(w2_raw[:], words_of(w2_words))
+        w2_raw_scales = new([P, N], U8, "w2_raw_scales", tag="table")
+        nc.vector.memset(w2_raw_scales[:].bitcast(I32), 0)
+        for q in range(QUADS):
+            load_scale_rows(nc.sync, w2_raw_scales, w2_scales, q)
+        w2_dealt = deal("w2_dealt", w2_raw, I32)
         y = [psum.tile([P, S], F32, name="y%d" % t, tag="y%d" % t) for t in range(PACK)]
         for t in range(PACK):
             rows = slice(t * P, (t + 1) * P)
@@ -105,37 +109,35 @@ def tile_picked_hashnormhinge_none_po_kernel(
                 rhs=x_picked[:].bitcast(FP8X4), rhs_scale=x_plane[:], start=True, stop=True,
             )
 
-        mirror = new([P, PACK, S], F32, "mirror")
-        denom = new([P, PACK, S], F32, "denom")
-        root = new([P, PACK, S], F32, "root")
+        size = new([P, PACK, S], F32, "size")
+        square = new([P, PACK, S], F32, "square")
+        inverse = new([P, PACK, S], F32, "inverse")
+        gained = new([P, PACK, S], F32, "gained")
         for t in range(PACK):
-            if t in SCALAR_ABS:
-                nc.scalar.activation(denom[:, t, :], y[t][:], ACT.Abs)
-                nc.scalar.activation(root[:, t, :], denom[:, t, :], ACT.Abs_reciprocal_sqrt, bias=0.5)
-            else:
-                nc.vector.tensor_scalar(mirror[:, t, :], y[t][:], -1.0, 0.5, ALU.mult, ALU.add)
-                nc.vector.scalar_tensor_tensor(denom[:, t, :], y[t][:], 0.5, mirror[:, t, :], ALU.add, ALU.max)
-                nc.scalar.activation(root[:, t, :], denom[:, t, :], ACT.Abs_reciprocal_sqrt)
+            nc.scalar.activation(size[:, t, :], y[t][:], ACT.Abs)
+            nc.vector.scalar_tensor_tensor(square[:, t, :], size[:, t, :], 1.0, size[:, t, :], ALU.add, ALU.mult)
+            nc.scalar.activation(inverse[:, t, :], square[:, t, :], ACT.Abs_reciprocal_sqrt, bias=0.25)
+        for t in range(PACK):
+            nc.vector.tensor_scalar_mul(gained[:, t, :], y[t][:], gn_sb[:, t : t + 1])
 
-        w2_plane = deal("w2_plane", w2_raw_scales, U8, tag="mirror")
-        w2_dealt = deal("w2_dealt", w2_raw, I32, tag="denom")
+        w2_plane = deal("w2_plane", w2_raw_scales, U8, tag="size")
 
         h_wide = new([P, (PACK + 1) * S], F32, "h_wide")
-        nc.gpsimd.memset(h_wide[:, PACK * S :], 0.0)
-        h_sb = h_wide[:, : PACK * S].rearrange("p (t j) -> p t j", t=PACK)
+        nc.vector.memset(h_wide[:, PACK * S :], 0.0)
+
+        def h_at(t):
+            return (PACK - 1 - t) * S
+
+        h = [psum.tile([P, S], F32, name="h%d" % t, tag="h%d" % t) for t in range(PACK)]
         for half in range(2):
-            root_at = new([P, PACK, HALF], F32, "root_at%d" % half)
-            part = new([P, PACK, HALF], F32, "part%d" % half)
+            inverse_at = new([P, PACK, HALF], F32, "inverse_at%d" % half)
             for t in range(PACK):
-                nc.scalar.activation(root_at[:, t, :], root[:, t, :].indirect(half_list(n1_sb, half)), ACT.Copy)
-                nc.vector.scalar_tensor_tensor(
-                    part[:, t, :], y[t][:, cols(half)], gn_sb[:, t : t + 1], root_at[:, t, :], ALU.mult, ALU.mult
-                )
-            z_bf = new([P, HALF, PACK], BF16, "z_bf%d" % half)
+                nc.scalar.activation(inverse_at[:, t, :], inverse[:, t, :].indirect(half_list(n1_sb, half)), ACT.Copy)
+            z_bf = new([P, HALF, PACK], BF16, "z_bf%d" % half, tag="z_bf")
             nc.vector.tensor_tensor(
                 z_bf[:].rearrange("p (c i) t -> p c t i", i=4),
-                part[:].rearrange("p t (c i) -> p c t i", i=4),
-                root_at[:].rearrange("p t (c i) -> p c t i", i=4),
+                gained[:, :, cols(half)].rearrange("p t (c i) -> p c t i", i=4),
+                inverse_at[:].rearrange("p t (c i) -> p c t i", i=4),
                 ALU.mult,
             )
             z_words = new([P, HALF], U32, "z_words%d" % half)
@@ -143,20 +145,17 @@ def tile_picked_hashnormhinge_none_po_kernel(
             nc.vector.quantize_mx(
                 out=z_words[:].bitcast(FP8X4), scales=z_plane[:], in_=z_bf[:].rearrange("p j t -> p (j t)")
             )
-            for pair in range(2):
-                bank = psum.tile([P, 2, HALF], F32, name="h%d%d" % (half, pair), tag="h%d%d" % (half, pair))
-                for e in range(2):
-                    t = 2 * pair + e
-                    rows = slice(t * P, (t + 1) * P)
-                    nc.tensor.matmul_mx(
-                        out=bank[:, e, :], lhsT=w2_dealt[:, rows].bitcast(FP8X4), lhsT_scale=w2_plane[:, rows],
-                        rhs=z_words[:].bitcast(FP8X4), rhs_scale=z_plane[:], start=True, stop=True,
-                    )
-                dest = h_sb[:, 2 * pair : 2 * pair + 2, cols(half)]
-                if half == 1 and pair == 1:
-                    nc.vector.tensor_copy(dest, bank[:])
+            for t in range(PACK):
+                rows = slice(t * P, (t + 1) * P)
+                nc.tensor.matmul_mx(
+                    out=h[t][:, cols(half)], lhsT=w2_dealt[:, rows].bitcast(FP8X4), lhsT_scale=w2_plane[:, rows],
+                    rhs=z_words[:].bitcast(FP8X4), rhs_scale=z_plane[:], start=True, stop=True,
+                )
+                dest = h_wide[:, h_at(t) + half * HALF : h_at(t) + (half + 1) * HALF]
+                if half == 1 and t > 1:
+                    nc.vector.tensor_copy(dest, h[t][:, cols(half)])
                 else:
-                    nc.scalar.copy(dest, bank[:])
+                    nc.scalar.copy(dest, h[t][:, cols(half)])
 
         out_rows = out_0.rearrange("(p t) j -> p t j", t=PACK)
         o_words = new([P, S], I32, "o_words")
@@ -169,7 +168,7 @@ def tile_picked_hashnormhinge_none_po_kernel(
             engine_copy(res_bf[:, js, ts], res[:, ts, js].rearrange("p t j -> p j t"))
 
         for t in range(PACK):
-            window = h_wide[:, t * S : (t + 2) * S]
+            window = h_wide[:, h_at(t) : h_at(t) + 2 * S]
             h2 = new([P, S], F32, "h2_%d" % t)
             h3 = new([P, S], F32, "h3_%d" % t)
             nc.scalar.activation(h3[:], window.indirect(n3_sb[:]), ACT.Copy, scale=0.5)
@@ -180,21 +179,20 @@ def tile_picked_hashnormhinge_none_po_kernel(
             down = new([P, S], F32, "down%d" % t)
             up = new([P, S], F32, "up%d" % t)
             down_pos = new([P, S], F32, "down_pos%d" % t)
-            nc.vector.scalar_tensor_tensor(up[:], h_sb[:, t, :], -0.5, h3[:], ALU.mult, ALU.add)
-            nc.vector.tensor_tensor(down[:], h_sb[:, t, :], h2[:], ALU.subtract)
+            nc.vector.scalar_tensor_tensor(up[:], h[t][:], -0.5, h3[:], ALU.mult, ALU.add)
+            nc.vector.tensor_tensor(down[:], h[t][:], h2[:], ALU.subtract)
             nc.vector.tensor_scalar_max(down_pos[:], up[:], 0.0)
             nc.vector.scalar_tensor_tensor(res[:, t, :], down[:], 0.0, down_pos[:], ALU.max, ALU.add)
             nc.sync.dma_start(out_rows[:, t, :], res[:, t, :])
-            if t == 1:
-                interleave(nc.scalar.copy, 0, slice(0, S))
-        for half in range(2):
-            interleave(nc.vector.tensor_copy, 1, cols(half))
+        interleave(nc.scalar.copy, 0, slice(0, S))
+        interleave(nc.vector.tensor_copy, 1, cols(0))
+        interleave(nc.scalar.copy, 1, cols(1))
         for half in range(2):
             nc.vector.quantize_mx(
                 out=o_words[:, cols(half)].bitcast(FP8X4), scales=o_plane[:, cols(half)],
                 in_=res_bf[:, cols(half), :].rearrange("p j t -> p (j t)"),
             )
-        nc.scalar.dma_start(words_of(out_1), o_words[:])
+            nc.scalar.dma_start(words_of(out_1)[:, cols(half)], o_words[:, cols(half)])
         for q in range(QUADS):
             queue = nc.sync if q < 3 else nc.scalar
             queue.dma_start(out_2[0].bitcast(I32)[4 * q : 4 * q + 4, :], o_plane[:].bitcast(I32)[32 * q : 32 * q + 4, :])

@@ -62,22 +62,20 @@ def tile_picked_hashnormhinge_none_po_kernel(
         nc.vector.memset(x_plane[:].bitcast(I32), 0)
 
         w1_raw = new([P, H], I32, "w1_raw")
-        w2_raw = new([P, N], I32, "w2_raw")
         x_table = new([P, T], I32, "x_table", tag="table")
         gn_sb = new([P, PACK], F32, "gn_sb")
         nc.sync.dma_start(offs_sb[:], offs)
         nc.scalar.dma_start(
             x_table_scales[:].bitcast(I32), x_scales[0].bitcast(I32).unsqueeze(1).to_broadcast([16, 8, T // 4])
         )
-        nc.sync.dma_start(x_table[:], words_of(x_words))
-        for q in range(QUADS):
-            load_scale_rows(nc.scalar if q < 2 else nc.gpsimd, w1_raw_scales, w1_scales, q)
         nc.scalar.dma_start(w1_raw[:], words_of(w1_words))
+        for q in range(QUADS):
+            load_scale_rows(nc.scalar if q == 0 else nc.sync, w1_raw_scales, w1_scales, q)
+        nc.scalar.dma_start(x_table[:], words_of(x_words))
         nc.sync.dma_start(n1_sb[:], n1)
         nc.sync.dma_start(n2_sb[:], n2)
         nc.sync.dma_start(n3_sb[:], n3)
-        nc.sync.dma_start(w2_raw[:], words_of(w2_words))
-        nc.sync.dma_start(gn_sb[:], gn.rearrange("(p t) o -> p (t o)", t=PACK))
+        nc.gpsimd.dma_start(gn_sb[:], gn.rearrange("(p t) o -> p (t o)", t=PACK))
 
         warm_in = new([P, 1], F32, "warm_in")
         warm_out = new([P, 1], F32, "warm_out")
@@ -87,7 +85,7 @@ def tile_picked_hashnormhinge_none_po_kernel(
         x_picked_scales = new([P, S], U8, "x_picked_scales")
         nc.vector.tensor_copy(x_picked_scales[:], x_table_scales[:].indirect(offs_sb[:]))
         for q in range(QUADS):
-            nc.scalar.dma_start(
+            nc.sync.dma_start(
                 x_plane[:].bitcast(I32)[32 * q : 32 * q + 4, :],
                 x_picked_scales[:].bitcast(I32)[32 * q : 32 * q + 32 : 8, :],
             )
@@ -96,11 +94,12 @@ def tile_picked_hashnormhinge_none_po_kernel(
         x_picked = new([P, S], U32, "x_picked")
         nc.vector.tensor_copy(x_picked[:], x_table[:].bitcast(U32).indirect(offs_sb[:]))
 
-        w2_raw_scales = new([P, N], U8, "w2_raw_scales", tag="table")
-        nc.vector.memset(w2_raw_scales[:].bitcast(I32), 0)
+        w2_raw = new([P, N], I32, "w2_raw", tag="table")
+        nc.scalar.dma_start(w2_raw[:], words_of(w2_words))
+        w2_raw_scales = new([P, N], U8, "w2_raw_scales", tag="w1_raw_scales")
+        nc.gpsimd.memset(w2_raw_scales[:].bitcast(U32), 0)
         for q in range(QUADS):
             load_scale_rows(nc.sync, w2_raw_scales, w2_scales, q)
-        w2_dealt = deal("w2_dealt", w2_raw, I32)
         y = [psum.tile([P, S], F32, name="y%d" % t, tag="y%d" % t) for t in range(PACK)]
         for t in range(PACK):
             rows = slice(t * P, (t + 1) * P)
@@ -121,6 +120,7 @@ def tile_picked_hashnormhinge_none_po_kernel(
             nc.vector.tensor_scalar_mul(gained[:, t, :], y[t][:], gn_sb[:, t : t + 1])
 
         w2_plane = deal("w2_plane", w2_raw_scales, U8, tag="size")
+        w2_dealt = deal("w2_dealt", w2_raw, I32, tag="square")
 
         h_wide = new([P, (PACK + 1) * S], F32, "h_wide")
         nc.vector.memset(h_wide[:, PACK * S :], 0.0)

@@ -14,7 +14,9 @@ ACT = mybir.ActivationFunctionType
 P = 128
 PACK = 4
 QUADS = 4
+BLOCKS = 16
 HALF = S // 2
+RUN = 4
 
 
 def words_of(packed):
@@ -66,7 +68,8 @@ def tile_picked_hashnormhinge_none_po_kernel(
         gn_sb = new([P, PACK], F32, "gn_sb")
         nc.sync.dma_start(offs_sb[:], offs)
         nc.scalar.dma_start(
-            x_table_scales[:].bitcast(I32), x_scales[0].bitcast(I32).unsqueeze(1).to_broadcast([16, 8, T // 4])
+            x_table_scales[:].bitcast(I32),
+            x_scales[0].bitcast(I32).unsqueeze(1).to_broadcast([BLOCKS, P // BLOCKS, T // 4]),
         )
         nc.scalar.dma_start(w1_raw[:], words_of(w1_words))
         for q in range(QUADS):
@@ -100,6 +103,7 @@ def tile_picked_hashnormhinge_none_po_kernel(
         nc.gpsimd.memset(w2_raw_scales[:].bitcast(U32), 0)
         for q in range(QUADS):
             load_scale_rows(nc.sync, w2_raw_scales, w2_scales, q)
+
         y = [psum.tile([P, S], F32, name="y%d" % t, tag="y%d" % t) for t in range(PACK)]
         for t in range(PACK):
             rows = slice(t * P, (t + 1) * P)
@@ -135,9 +139,9 @@ def tile_picked_hashnormhinge_none_po_kernel(
                 nc.scalar.activation(inverse_at[:, t, :], inverse[:, t, :].indirect(half_list(n1_sb, half)), ACT.Copy)
             z_bf = new([P, HALF, PACK], BF16, "z_bf%d" % half, tag="z_bf")
             nc.vector.tensor_tensor(
-                z_bf[:].rearrange("p (c i) t -> p c t i", i=4),
-                gained[:, :, cols(half)].rearrange("p t (c i) -> p c t i", i=4),
-                inverse_at[:].rearrange("p t (c i) -> p c t i", i=4),
+                z_bf[:].rearrange("p (c i) t -> p c t i", i=RUN),
+                gained[:, :, cols(half)].rearrange("p t (c i) -> p c t i", i=RUN),
+                inverse_at[:].rearrange("p t (c i) -> p c t i", i=RUN),
                 ALU.mult,
             )
             z_words = new([P, HALF], U32, "z_words%d" % half)
@@ -152,7 +156,7 @@ def tile_picked_hashnormhinge_none_po_kernel(
                     rhs=z_words[:].bitcast(FP8X4), rhs_scale=z_plane[:], start=True, stop=True,
                 )
                 dest = h_wide[:, h_at(t) + half * HALF : h_at(t) + (half + 1) * HALF]
-                if half == 1 and t > 1:
+                if half == 1 and t == PACK - 1:
                     nc.vector.tensor_copy(dest, h[t][:, cols(half)])
                 else:
                     nc.scalar.copy(dest, h[t][:, cols(half)])
@@ -170,20 +174,27 @@ def tile_picked_hashnormhinge_none_po_kernel(
         for t in range(PACK):
             window = h_wide[:, h_at(t) : h_at(t) + 2 * S]
             h2 = new([P, S], F32, "h2_%d" % t)
-            h3 = new([P, S], F32, "h3_%d" % t)
-            nc.scalar.activation(h3[:], window.indirect(n3_sb[:]), ACT.Copy, scale=0.5)
+            h3_halved = new([P, S], F32, "h3_halved%d" % t)
+            nc.scalar.activation(h3_halved[:], window.indirect(n3_sb[:]), ACT.Copy, scale=0.5)
             if t == 0:
                 nc.vector.tensor_copy(h2[:], window.indirect(n2_sb[:]))
+            elif t == 1:
+                nc.vector.tensor_copy(h2[:, cols(0)], window.indirect(half_list(n2_sb, 0)))
+                nc.scalar.activation(h2[:, cols(1)], window.indirect(half_list(n2_sb, 1)), ACT.Copy)
             else:
                 nc.scalar.activation(h2[:], window.indirect(n2_sb[:]), ACT.Copy)
             down = new([P, S], F32, "down%d" % t)
             up = new([P, S], F32, "up%d" % t)
-            down_pos = new([P, S], F32, "down_pos%d" % t)
-            nc.vector.scalar_tensor_tensor(up[:], h[t][:], -0.5, h3[:], ALU.mult, ALU.add)
-            nc.vector.tensor_tensor(down[:], h[t][:], h2[:], ALU.subtract)
-            nc.vector.tensor_scalar_max(down_pos[:], up[:], 0.0)
-            nc.vector.scalar_tensor_tensor(res[:, t, :], down[:], 0.0, down_pos[:], ALU.max, ALU.add)
+            up_pos = new([P, S], F32, "up_pos%d" % t)
+            nc.vector.scalar_tensor_tensor(up[:], h[t][:], -0.5, h3_halved[:], ALU.mult, ALU.add)
+            if t < PACK - 1:
+                nc.vector.tensor_tensor(down[:], h[t][:], h2[:], ALU.subtract)
+            nc.vector.tensor_scalar_max(up_pos[:], up[:], 0.0)
+            if t == PACK - 1:
+                nc.vector.tensor_tensor(down[:], h[t][:], h2[:], ALU.subtract)
+            nc.vector.scalar_tensor_tensor(res[:, t, :], down[:], 0.0, up_pos[:], ALU.max, ALU.add)
             nc.sync.dma_start(out_rows[:, t, :], res[:, t, :])
+
         interleave(nc.scalar.copy, 0, slice(0, S))
         interleave(nc.vector.tensor_copy, 1, cols(0))
         interleave(nc.scalar.copy, 1, cols(1))
@@ -194,5 +205,5 @@ def tile_picked_hashnormhinge_none_po_kernel(
             )
             nc.scalar.dma_start(words_of(out_1)[:, cols(half)], o_words[:, cols(half)])
         for q in range(QUADS):
-            queue = nc.sync if q < 3 else nc.scalar
+            queue = nc.sync if q < QUADS - 1 else nc.scalar
             queue.dma_start(out_2[0].bitcast(I32)[4 * q : 4 * q + 4, :], o_plane[:].bitcast(I32)[32 * q : 32 * q + 4, :])

from contextlib import ExitStack

import concourse.mybir as mybir

K, T, S, H, N = 512, 2048, 256, 512, 512
FLOPS = 2 * K * H * S + 2 * H * N * S

F32, BF16 = mybir.dt.float32, mybir.dt.bfloat16
I32, U32, U16, U8 = mybir.dt.int32, mybir.dt.uint32, mybir.dt.uint16, mybir.dt.uint8
FP8X4 = mybir.dt.float8_e4m3fn_x4
ALU = mybir.AluOpType
ACT = mybir.ActivationFunctionType

P = 128
PACK = 4
QUADS = 4
BLOCKS = 16
HALF = S // 2
RUN = 4


def words_of(packed):
    return packed[0].rearrange("p n t -> p (n t)").bitcast(I32)


def tile_picked_hashnormhinge_none_po_kernel(
    tc, x_words, x_scales, w1_words, w1_scales, gn, w2_words, w2_scales, offs, n1, n2, n3, out_0, out_1, out_2
):
    nc = tc.nc
    with ExitStack() as ctx:
        lists = ctx.enter_context(tc.tile_pool(name="lists", bufs=1))
        sb = ctx.enter_context(tc.tile_pool(name="sb", bufs=1))
        psum = ctx.enter_context(tc.psum_pool(name="psum", bufs=1))

        def new(shape, dtype, name, tag=None):
            return sb.tile(shape, dtype, name=name, tag=tag or name, align_bytes=64)

        offs_sb = lists.tile([P, S // 16], U16, name="offs_sb")
        n1_sb = lists.tile([P, S // 16], U16, name="n1_sb")
        n2_sb = lists.tile([P, S // 16], U16, name="n2_sb")
        n3_sb = lists.tile([P, S // 16], U16, name="n3_sb")

        def half_list(tile, half):
            return tile[:, half * (HALF // 16) : (half + 1) * (HALF // 16)]

        def cols(half):
            return slice(half * HALF, (half + 1) * HALF)

        def load_scale_rows(queue, tile, scales, q):
            rows = scales[0].bitcast(I32)[4 * q : 4 * q + 4, :]
            queue.dma_start(tile[:].bitcast(I32)[32 * q : 32 * q + 4, :], rows)

        def deal(name, raw, dtype, tag=None):
            dealt = new([P, H], dtype, name, tag=tag)
            nc.vector.tensor_copy(
                dealt[:].rearrange("p (t m) -> p m t", t=PACK), raw[:].rearrange("p (m t) -> p m t", t=PACK)
            )
            return dealt

        x_table_scales = new([P, T], U8, "x_table_scales")
        w1_raw_scales = new([P, H], U8, "w1_raw_scales")
        x_plane = new([P, S], U8, "x_plane")
        nc.gpsimd.memset(w1_raw_scales[:].bitcast(U32), 0)
        nc.vector.memset(x_plane[:].bitcast(I32), 0)

        w1_raw = new([P, H], I32, "w1_raw")
        x_table = new([P, T], I32, "x_table", tag="table")
        gn_sb = new([P, PACK], F32, "gn_sb")
        nc.sync.dma_start(offs_sb[:], offs)
        nc.scalar.dma_start(
            x_table_scales[:].bitcast(I32),
            x_scales[0].bitcast(I32).unsqueeze(1).to_broadcast([BLOCKS, P // BLOCKS, T // 4]),
        )
        nc.scalar.dma_start(w1_raw[:], words_of(w1_words))
        for q in range(QUADS):
            load_scale_rows(nc.scalar if q == 0 else nc.sync, w1_raw_scales, w1_scales, q)
        nc.scalar.dma_start(x_table[:], words_of(x_words))
        nc.sync.dma_start(n1_sb[:], n1)
        nc.sync.dma_start(n2_sb[:], n2)
        nc.sync.dma_start(n3_sb[:], n3)
        nc.gpsimd.dma_start(gn_sb[:], gn.rearrange("(p t) o -> p (t o)", t=PACK))

        warm_in = new([P, 1], F32, "warm_in")
        warm_out = new([P, 1], F32, "warm_out")
        nc.vector.memset(warm_in[:], 1.0)
        nc.scalar.activation(warm_out[:], warm_in[:], ACT.Abs_reciprocal_sqrt)

        x_picked_scales = new([P, S], U8, "x_picked_scales")
        nc.vector.tensor_copy(x_picked_scales[:], x_table_scales[:].indirect(offs_sb[:]))
        for q in range(QUADS):
            nc.sync.dma_start(
                x_plane[:].bitcast(I32)[32 * q : 32 * q + 4, :],
                x_picked_scales[:].bitcast(I32)[32 * q : 32 * q + 32 : 8, :],
            )
        w1_dealt = deal("w1_dealt", w1_raw, I32)
        w1_plane = deal("w1_plane", w1_raw_scales, U8)
        x_picked = new([P, S], U32, "x_picked")
        nc.vector.tensor_copy(x_picked[:], x_table[:].bitcast(U32).indirect(offs_sb[:]))

        w2_raw = new([P, N], I32, "w2_raw", tag="table")
        nc.scalar.dma_start(w2_raw[:], words_of(w2_words))
        w2_raw_scales = new([P, N], U8, "w2_raw_scales", tag="w1_raw_scales")
        nc.gpsimd.memset(w2_raw_scales[:].bitcast(U32), 0)
        for q in range(QUADS):
            load_scale_rows(nc.sync, w2_raw_scales, w2_scales, q)

        y = [psum.tile([P, S], F32, name="y%d" % t, tag="y%d" % t) for t in range(PACK)]
        for t in range(PACK):
            rows = slice(t * P, (t + 1) * P)
            nc.tensor.matmul_mx(
                out=y[t][:], lhsT=w1_dealt[:, rows].bitcast(FP8X4), lhsT_scale=w1_plane[:, rows],
                rhs=x_picked[:].bitcast(FP8X4), rhs_scale=x_plane[:], start=True, stop=True,
            )

        size = new([P, PACK, S], F32, "size")
        square = new([P, PACK, S], F32, "square")
        inverse = new([P, PACK, S], F32, "inverse")
        gained = new([P, PACK, S], F32, "gained")
        for t in range(PACK):
            nc.scalar.activation(size[:, t, :], y[t][:], ACT.Abs)
            nc.vector.scalar_tensor_tensor(square[:, t, :], size[:, t, :], 1.0, size[:, t, :], ALU.add, ALU.mult)
            nc.scalar.activation(inverse[:, t, :], square[:, t, :], ACT.Abs_reciprocal_sqrt, bias=0.25)
        for t in range(PACK):
            nc.vector.tensor_scalar_mul(gained[:, t, :], y[t][:], gn_sb[:, t : t + 1])

        w2_plane = deal("w2_plane", w2_raw_scales, U8, tag="size")
        w2_dealt = deal("w2_dealt", w2_raw, I32, tag="square")

        h_wide = new([P, (PACK + 1) * S], F32, "h_wide")
        nc.vector.memset(h_wide[:, PACK * S :], 0.0)

        def h_at(t):
            return (PACK - 1 - t) * S

        h = [psum.tile([P, S], F32, name="h%d" % t, tag="h%d" % t) for t in range(PACK)]
        for half in range(2):
            inverse_at = new([P, PACK, HALF], F32, "inverse_at%d" % half)
            for t in range(PACK):
                nc.scalar.activation(inverse_at[:, t, :], inverse[:, t, :].indirect(half_list(n1_sb, half)), ACT.Copy)
            z_bf = new([P, HALF, PACK], BF16, "z_bf%d" % half, tag="z_bf")
            nc.vector.tensor_tensor(
                z_bf[:].rearrange("p (c i) t -> p c t i", i=RUN),
                gained[:, :, cols(half)].rearrange("p t (c i) -> p c t i", i=RUN),
                inverse_at[:].rearrange("p t (c i) -> p c t i", i=RUN),
                ALU.mult,
            )
            z_words = new([P, HALF], U32, "z_words%d" % half)
            z_plane = new([P, HALF], U8, "z_plane%d" % half)
            nc.vector.quantize_mx(
                out=z_words[:].bitcast(FP8X4), scales=z_plane[:], in_=z_bf[:].rearrange("p j t -> p (j t)")
            )
            for t in range(PACK):
                rows = slice(t * P, (t + 1) * P)
                nc.tensor.matmul_mx(
                    out=h[t][:, cols(half)], lhsT=w2_dealt[:, rows].bitcast(FP8X4), lhsT_scale=w2_plane[:, rows],
                    rhs=z_words[:].bitcast(FP8X4), rhs_scale=z_plane[:], start=True, stop=True,
                )
                dest = h_wide[:, h_at(t) + half * HALF : h_at(t) + (half + 1) * HALF]
                if half == 1 and t == PACK - 1:
                    nc.vector.tensor_copy(dest, h[t][:, cols(half)])
                else:
                    nc.scalar.copy(dest, h[t][:, cols(half)])

        out_rows = out_0.rearrange("(p t) j -> p t j", t=PACK)
        o_words = new([P, S], I32, "o_words")
        o_plane = new([P, S], U8, "o_plane")
        res = new([P, PACK, S], F32, "res")
        res_bf = new([P, S, PACK], BF16, "res_bf")

        def interleave(engine_copy, pair, js):
            ts = slice(2 * pair, 2 * pair + 2)
            engine_copy(res_bf[:, js, ts], res[:, ts, js].rearrange("p t j -> p j t"))

        for t in range(PACK):
            window = h_wide[:, h_at(t) : h_at(t) + 2 * S]
            h2 = new([P, S], F32, "h2_%d" % t)
            h3_halved = new([P, S], F32, "h3_halved%d" % t)
            nc.scalar.activation(h3_halved[:], window.indirect(n3_sb[:]), ACT.Copy, scale=0.5)
            if t == 0:
                nc.vector.tensor_copy(h2[:], window.indirect(n2_sb[:]))
            elif t == 1:
                nc.vector.tensor_copy(h2[:, cols(0)], window.indirect(half_list(n2_sb, 0)))
                nc.scalar.activation(h2[:, cols(1)], window.indirect(half_list(n2_sb, 1)), ACT.Copy)
            else:
                nc.scalar.activation(h2[:], window.indirect(n2_sb[:]), ACT.Copy)
            down = new([P, S], F32, "down%d" % t)
            up = new([P, S], F32, "up%d" % t)
            up_pos = new([P, S], F32, "up_pos%d" % t)
            nc.vector.scalar_tensor_tensor(up[:], h[t][:], -0.5, h3_halved[:], ALU.mult, ALU.add)
            if t < PACK - 1:
                nc.vector.tensor_tensor(down[:], h[t][:], h2[:], ALU.subtract)
            nc.vector.tensor_scalar_max(up_pos[:], up[:], 0.0)
            if t == PACK - 1:
                nc.vector.tensor_tensor(down[:], h[t][:], h2[:], ALU.subtract)
            nc.vector.scalar_tensor_tensor(res[:, t, :], down[:], 0.0, up_pos[:], ALU.max, ALU.add)
            nc.sync.dma_start(out_rows[:, t, :], res[:, t, :])

        interleave(nc.scalar.copy, 0, slice(0, S))
        interleave(nc.vector.tensor_copy, 1, cols(0))
        interleave(nc.scalar.copy, 1, cols(1))
        for half in range(2):
            nc.vector.quantize_mx(
                out=o_words[:, cols(half)].bitcast(FP8X4), scales=o_plane[:, cols(half)],
                in_=res_bf[:, cols(half), :].rearrange("p j t -> p (j t)"),
            )
            nc.scalar.dma_start(words_of(out_1)[:, cols(half)], o_words[:, cols(half)])
        for q in range(QUADS):
            queue = nc.sync if q < QUADS - 1 else nc.scalar
            queue.dma_start(out_2[0].bitcast(I32)[4 * q : 4 * q + 4, :], o_plane[:].bitcast(I32)[32 * q : 32 * q + 4, :])
